import numpy as np
import ml_dtypes


def mxq(x, axis, fmt="e4m3"):
    dtype, down = {"e4m3": (ml_dtypes.float8_e4m3fn, 7), "e5m2": (ml_dtypes.float8_e5m2, 14)}[fmt]
    v = np.moveaxis(np.asarray(x, np.float32).astype(ml_dtypes.bfloat16).astype(np.float64), axis, -1)
    blocks = v.reshape(v.shape[:-1] + (-1, 32))
    amax = np.abs(blocks).max(-1, keepdims=True)
    byte = np.maximum(np.where(amax > 0, np.frexp(amax)[1] - 1 + 127, 0) - down, 1)
    scale = np.exp2(byte - 127.0)
    codes = (blocks / scale).astype(np.float32).astype(dtype).astype(np.float64)
    return np.moveaxis((codes * scale).reshape(v.shape), -1, axis)


WIDE = False


def mx_kscale(k):
    if not WIDE:
        return np.ones(k)
    levels = np.array([10, -10, 5, -5, 0])
    if k % 512:
        return np.exp2(np.random.permutation(np.resize(levels, k // 32))).repeat(32)
    a = np.empty((k // 512, 16))
    for p in range(k // 512):
        a[p, :8] = np.random.permutation(np.resize(levels, 8))
        for g in range(8):
            far = levels[np.abs(levels - a[p, g]) >= 10]
            a[p, g + 8] = far[np.random.randint(len(far))]
    return np.exp2(a.ravel()).repeat(32)


def f64(x):
    return np.asarray(x).astype(np.float64)


def striped(idx):
    return np.tile(np.asarray(idx).reshape(-1, 16).T, (8, 1)).astype(np.uint16)


def unstriped(offs):
    return offs[:16].T.reshape(-1).astype(np.int64)


E2M1 = np.array([0.0, 0.5, 1.0, 1.5, 2.0, 3.0, 4.0, 6.0, -0.0, -0.5, -1.0, -1.5, -2.0, -3.0, -4.0, -6.0])


def pack_weight(w, fmt):
    k, n = w.shape
    w = f64(np.asarray(w, np.float32).astype(ml_dtypes.bfloat16)).reshape(k // 32, 32, n)
    amax = np.abs(w).max(1)
    if fmt == "e4m3":
        byte = np.frexp(amax)[1] - 1 + 127 - 7
    else:
        mant, ex = np.frexp(amax / 6.0)
        byte = np.where(mant > 0.5, ex, ex - 1) + 127
    byte = np.clip(np.where(amax > 0, byte, 1), 1, 254)
    scaled = (w * np.exp2(127.0 - byte)[:, None, :]).reshape(k, n).astype(np.float32)
    by_word = np.ascontiguousarray(scaled.reshape(k // 512, 128, 4, n).transpose(0, 1, 3, 2))
    if fmt == "e4m3":
        words = by_word.astype(ml_dtypes.float8_e4m3fn).view(np.uint8)
    else:
        c = by_word.astype(ml_dtypes.float4_e2m1fn).view(np.uint8) & 0xF
        words = (c[..., 0::2] | (c[..., 1::2] << 4)).reshape(k // 512, 128, 2 * n)
    return np.ascontiguousarray(words), np.ascontiguousarray(byte.astype(np.uint8).reshape(k // 512, 16, n))


def unpack_weight(words, scales, fmt):
    g, _, n = scales.shape
    words = np.ascontiguousarray(words).reshape(g, 128, n, -1)
    if fmt == "e4m3":
        vals = words.view(ml_dtypes.float8_e4m3fn).astype(np.float64)
    else:
        nib = np.empty((g, 128, n, 4), np.uint8)
        nib[..., 0::2] = words & 0xF
        nib[..., 1::2] = words >> 4
        vals = E2M1[nib]
    vals = vals * np.repeat(np.exp2(scales.astype(np.float64) - 127.0), 8, axis=1)[..., None]
    return vals.transpose(0, 1, 3, 2).reshape(g * 512, n)


K, R, F, T, J, G = 512, 256, 512, 2048, 512, 32


def setup_inputs():
    n = np.random.standard_normal
    idx = np.random.permutation(T)[:J]
    fk = mx_kscale(K)
    ff = mx_kscale(F)
    tabp = pack_weight(n((K, T)) / fk[:, None], "e2m1")
    return {
        "tab_words": tabp[0],
        "tab_scales": tabp[1],
        "w1": (n((K, R)) * 1 / np.sqrt(K) * fk[:, None]).astype(np.float32),
        "gain": (np.random.uniform(0.5, 1.5, (R, 1))).astype(np.float32),
        "bias": (np.random.uniform(-0.5, 0.5, (R, 1))).astype(np.float32),
        "wo": (n((F, R)) * 1 / np.sqrt(F) * ff[:, None]).astype(np.float32),
        "dy": (n((F, J)) / ff[:, None]).astype(np.float32),
        "old": (0.5 * n((R, J))).astype(np.float32),
        "offs": striped(idx),
    }


def reference(tab_words, tab_scales, w1, gain, bias, wo, dy, old, offs):
    idx = unstriped(offs)
    tabu = unpack_weight(tab_words, tab_scales, "e2m1")
    w1q = mxq(f64(w1), 0, "e4m3")
    tabidxg = tabu[:, idx]
    a = w1q.T @ tabidxg
    m1 = a.reshape(R, G, J // G).mean(axis=2)
    mr = np.repeat(m1, J // G, axis=1)
    ce = a - mr
    v1 = np.sqrt(np.square(ce).reshape(R, G, J // G).mean(axis=2) + 0.05)
    vr = np.repeat(v1, J // G, axis=1)
    s = ce / vr * f64(gain) + f64(bias)
    u1 = np.tanh(s)
    woq = mxq(f64(wo), 0, "e4m3")
    dyq = mxq(f64(dy), 0, "e4m3")
    c0 = woq.T @ dyq
    ds = c0 * (1.0 - np.square(u1))
    dvr = ds * f64(gain) * ce / np.square(vr) * (-1.0)
    dv1 = dvr.reshape(R, G, J // G).sum(axis=2)
    e1 = dv1 * 0.5 / np.sqrt(np.square(ce).reshape(R, G, J // G).mean(axis=2) + 0.05) / 16.0
    r1 = np.repeat(e1, J // G, axis=1)
    dce = ds * f64(gain) / vr + r1 * ce * 2.0
    dmr = dce * (-1.0)
    dm1 = dmr.reshape(R, G, J // G).sum(axis=2)
    e2 = dm1 / 16.0
    r2 = np.repeat(e2, J // G, axis=1)
    da = dce + r2
    y = da + f64(old)
    return y

@@ -1,0 +1,204 @@
+from contextlib import ExitStack
+
+import concourse.mybir as mybir
+
+K, R, F, T, J = 512, 256, 512, 2048, 512
+FLOPS = 2 * K * R * J + 2 * F * R * J
+
+F32 = mybir.dt.float32
+BF16 = mybir.dt.bfloat16
+I32 = mybir.dt.int32
+U32 = mybir.dt.uint32
+U16 = mybir.dt.uint16
+U8 = mybir.dt.uint8
+FP8X4 = mybir.dt.float8_e4m3fn_x4
+FP4X4 = mybir.dt.float4_e2m1fn_x4
+ALU = mybir.AluOpType
+ACT = mybir.ActivationFunctionType
+AX = mybir.AxisListType
+
+P = 128
+PACK = 4
+H = R // P
+GS = 16
+NC = 2
+CW = J // NC
+CG = CW // GS
+EPS = 0.05
+
+
+def interleave(engine_copy, dst, src):
+    engine_copy(dst.rearrange("p (c i) t -> p c t i", i=4), src.rearrange("p t (c i) -> p c t i", i=4))
+
+
+def tile_attend_cgroupscale_kernel(tc, tab_words, tab_scales, w1, gain, bias, wo, dy, old, offs, out):
+    nc = tc.nc
+    with ExitStack() as ctx:
+        sb = ctx.enter_context(tc.tile_pool(name="sb", bufs=1))
+        ps = ctx.enter_context(tc.psum_pool(name="ps", bufs=1))
+
+        def tile(name, shape, dtype):
+            return sb.tile(shape, dtype, name=name, align_bytes=64)
+
+        offsets = sb.tile([P, J // 16], U16, name="offsets")
+        words = tile("words", [P, T], U16)
+        scales = tile("scales", [P, T], U8)
+        w1_raw = tile("w1_raw", [P, PACK, R], F32)
+        wo_raw = tile("wo_raw", [P, PACK, R], F32)
+        dy_raw = [tile(f"dy_raw{c}", [P, PACK, CW], F32) for c in range(NC)]
+        old_sb = [tile(f"old{c}", [P, H, CW], F32) for c in range(NC)]
+        gain_sb = tile("gain_sb", [P, H], F32)
+        bias_sb = tile("bias_sb", [P, H], F32)
+
+        nc.gpsimd.memset(scales[:].bitcast(I32), 0)
+        warm = tile("warm", [P, 1], F32)
+        warm_out = tile("warm_out", [P, 1], F32)
+        nc.gpsimd.memset(warm[:], 1.0)
+        nc.scalar.activation(warm_out[:], warm[:], ACT.Abs_reciprocal_sqrt)
+
+        def load_scales():
+            for q in range(4):
+                nc.sync.dma_start(scales[32 * q : 32 * q + 4, :].bitcast(I32), tab_scales[0, 4 * q : 4 * q + 4, :].bitcast(I32))
+
+        nc.sync.dma_start(offsets[:], offs)
+        load_scales()
+        nc.sync.dma_start(w1_raw[:], w1.rearrange("(p t) r -> p t r", t=PACK))
+        nc.sync.dma_start(words[:].bitcast(I32), tab_words[0].bitcast(I32))
+        nc.sync.dma_start(wo_raw[:], wo.rearrange("(p t) r -> p t r", t=PACK))
+        dy_v = dy.rearrange("(p t) j -> p t j", t=PACK)
+        for c in range(NC):
+            nc.sync.dma_start(dy_raw[c][:], dy_v[:, :, c * CW : (c + 1) * CW])
+        with nc.allow_non_contiguous_dma(reason="one value a partition"):
+            nc.sync.dma_start(gain_sb[:], gain.rearrange("(h p) o -> p (h o)", p=P))
+            nc.sync.dma_start(bias_sb[:], bias.rearrange("(h p) o -> p (h o)", p=P))
+        old_v = old.rearrange("(h p) j -> p h j", p=P)
+        for c in range(NC):
+            nc.sync.dma_start(old_sb[c][:], old_v[:, :, c * CW : (c + 1) * CW])
+
+        def quantize(name, grouped, width):
+            codes = tile(name + "_codes", [P, width], U32)
+            plane = tile(name + "_plane", [P, width], U8)
+            nc.vector.quantize_mx(codes[:].bitcast(FP8X4), plane[:], grouped[:].rearrange("p w t -> p (w t)"))
+            return codes, plane
+
+        w1_bf = tile("w1_bf", [P, R, PACK], BF16)
+        interleave(nc.scalar.copy, w1_bf[:], w1_raw[:])
+        g_scales, g_words = [], []
+        for c in range(NC):
+            gs = tile(f"g_scales{c}", [P, CW], U8)
+            nc.vector.tensor_copy(gs[:], scales[:].indirect(offsets[:, c * CW // 16 : (c + 1) * CW // 16]))
+            g_scales.append(gs)
+        w1_codes, w1_plane = quantize("w1", w1_bf, R)
+        for c in range(NC):
+            gw = tile(f"g_words{c}", [P, CW], U16)
+            nc.vector.tensor_copy(gw[:], words[:].indirect(offsets[:, c * CW // 16 : (c + 1) * CW // 16]))
+            g_words.append(gw)
+        a_ps = [ps.tile([P, H, CW], F32, name=f"a_ps{c}") for c in range(NC)]
+        for c in range(NC):
+            for h in range(H):
+                nc.tensor.matmul_mx(
+                    a_ps[c][:, h, :],
+                    lhsT=w1_codes[:, h * P : (h + 1) * P].bitcast(FP8X4),
+                    lhsT_scale=w1_plane[:, h * P : (h + 1) * P],
+                    rhs=g_words[c][:].bitcast(FP4X4),
+                    rhs_scale=g_scales[c][:],
+                    start=True,
+                    stop=True,
+                )
+
+        wo_bf = tile("wo_bf", [P, R, PACK], BF16)
+        interleave(nc.scalar.copy, wo_bf[:], wo_raw[:])
+        dy_bf = [tile(f"dy_bf{c}", [P, CW, PACK], BF16) for c in range(NC)]
+        for c in range(NC):
+            interleave(nc.scalar.copy, dy_bf[c][:], dy_raw[c][:])
+
+        NG = H * CG
+        stats, rstd = [], []
+        for c in range(NC):
+            st = tile(f"stats{c}", [P, NG, 3], F32)
+            flat = a_ps[c][:].rearrange("p h j -> p (h j)")
+            for n in range(NG // 2):
+                nc.vector.bn_stats(
+                    st[:, 2 * n : 2 * n + 2, :].rearrange("p g s -> p (g s)"),
+                    flat[:, 2 * n * GS : (2 * n + 2) * GS].rearrange("p (g i) -> p i g", g=2),
+                )
+            rs = tile(f"rstd{c}", [P, NG], F32)
+            nc.scalar.activation(rs[:], st[:, :, 2], ACT.Abs_reciprocal_sqrt, bias=EPS, scale=1.0 / GS)
+            stats.append(st)
+            rstd.append(rs)
+
+        def by_group(ap):
+            return ap.rearrange("p (g i) -> p g i", i=GS)
+
+        def spread(ap):
+            return ap.unsqueeze(2).to_broadcast([P, ap.shape[1], GS])
+
+        ce = []
+        for c in range(NC):
+            t = tile(f"ce{c}", [P, H * CW], F32)
+            nc.vector.tensor_tensor(
+                by_group(t[:]), by_group(a_ps[c][:].rearrange("p h j -> p (h j)")), spread(stats[c][:, :, 1]), ALU.subtract
+            )
+            ce.append(t)
+        xh = []
+        for c in range(NC):
+            x = tile(f"xh{c}", [P, H * CW], F32)
+            nc.vector.tensor_tensor(by_group(x[:]), by_group(ce[c][:]), spread(rstd[c][:]), ALU.mult)
+            xh.append(x)
+
+        wo_codes, wo_plane = quantize("wo", wo_bf, R)
+        c_ps = [ps.tile([P, H, CW], F32, name=f"c_ps{c}") for c in range(NC)]
+        for c in range(NC):
+            dy_codes, dy_plane = quantize(f"dy{c}", dy_bf[c], CW)
+            for h in range(H):
+                nc.tensor.matmul_mx(
+                    c_ps[c][:, h, :],
+                    lhsT=wo_codes[:, h * P : (h + 1) * P].bitcast(FP8X4),
+                    lhsT_scale=wo_plane[:, h * P : (h + 1) * P],
+                    rhs=dy_codes[:].bitcast(FP8X4),
+                    rhs_scale=dy_plane[:],
+                    start=True,
+                    stop=True,
+                )
+
+        pieces = [(c, h) for c in range(NC) for h in range(H)]
+        u2, scaled = {}, {}
+        for c, h in pieces:
+            cols = slice(h * CW, (h + 1) * CW)
+            u = tile(f"u{c}{h}", [P, CW], F32)
+            nc.scalar.activation(u[:], xh[c][:, cols], ACT.Tanh, bias=bias_sb[:, h : h + 1], scale=gain_sb[:, h : h + 1])
+            u2[c, h] = tile(f"u2{c}{h}", [P, CW], F32)
+            nc.scalar.activation(u2[c, h][:], u[:], ACT.Square)
+        for c, h in pieces:
+            scaled[c, h] = tile(f"cs{c}{h}", [P, CW], F32)
+            nc.vector.scalar_tensor_tensor(
+                by_group(scaled[c, h][:]),
+                by_group(c_ps[c][:, h, :]),
+                gain_sb[:, h : h + 1],
+                spread(rstd[c][:, h * CG : (h + 1) * CG]),
+                ALU.mult,
+                ALU.mult,
+            )
+        dps, backs = {}, {}
+        for c, h in pieces:
+            x = xh[c][:, h * CW : (h + 1) * CW]
+            dp = tile(f"dp{c}{h}", [P, 2, CW], F32)
+            nc.vector.scalar_tensor_tensor(dp[:, 0, :], u2[c, h][:], -1.0, scaled[c, h][:], ALU.add, ALU.mult)
+            nc.vector.tensor_tensor(dp[:, 1, :], dp[:, 0, :], x, ALU.mult)
+            sums = tile(f"sums{c}{h}", [P, 2 * CG], F32)
+            nc.vector.tensor_reduce(sums[:], dp[:].rearrange("p q (g i) -> p (q g) i", i=GS), AX.X, ALU.add)
+            back = tile(f"back{c}{h}", [P, CW], F32)
+            for g in range(CG):
+                cols = slice(g * GS, (g + 1) * GS)
+                nc.scalar.activation(
+                    back[:, cols], x[:, cols], ACT.Identity, bias=sums[:, g : g + 1], scale=sums[:, CG + g : CG + g + 1]
+                )
+            dps[c, h], backs[c, h] = dp, back
+        directs = {}
+        for c, h in pieces:
+            directs[c, h] = tile(f"direct{c}{h}", [P, CW], F32)
+            nc.vector.tensor_tensor(directs[c, h][:], old_sb[c][:, h, :], dps[c, h][:, 0, :], ALU.subtract)
+        for c, h in pieces:
+            y = tile(f"y{c}{h}", [P, CW], F32)
+            nc.vector.scalar_tensor_tensor(y[:], backs[c, h][:], 1.0 / GS, directs[c, h][:], ALU.mult, ALU.add)
+            nc.sync.dma_start(out[h * P : (h + 1) * P, c * CW : (c + 1) * CW], y[:])

@@ -37,22 +37,20 @@ def tile_attend_cgroupscale_kernel(tc, tab_words, tab_scales, w1, gain, bias, wo
         sb = ctx.enter_context(tc.tile_pool(name="sb", bufs=1))
         ps = ctx.enter_context(tc.psum_pool(name="ps", bufs=1))
 
-        def tile(name, shape, dtype):
-            return sb.tile(shape, dtype, name=name, align_bytes=64)
+        def tile(name, shape, dtype, slot=None):
+            return sb.tile(shape, dtype, name=name, tag=slot or name, align_bytes=64)
 
         offsets = sb.tile([P, J // 16], U16, name="offsets")
         words = tile("words", [P, T], U16)
         scales = tile("scales", [P, T], U8)
         w1_raw = tile("w1_raw", [P, PACK, R], F32)
-        wo_raw = tile("wo_raw", [P, PACK, R], F32)
-        dy_raw = [tile(f"dy_raw{c}", [P, PACK, CW], F32) for c in range(NC)]
-        old_sb = [tile(f"old{c}", [P, H, CW], F32) for c in range(NC)]
         gain_sb = tile("gain_sb", [P, H], F32)
         bias_sb = tile("bias_sb", [P, H], F32)
 
-        nc.gpsimd.memset(scales[:].bitcast(I32), 0)
-        warm = tile("warm", [P, 1], F32)
-        warm_out = tile("warm_out", [P, 1], F32)
+        nc.gpsimd.memset(scales[:, : T // 2].bitcast(I32), 0)
+        nc.vector.memset(scales[:, T // 2 :].bitcast(I32), 0)
+        warm = tile("warm", [P, 1], F32, slot="wo_raw")
+        warm_out = tile("warm_out", [P, 1], F32, slot="dy_raw")
         nc.gpsimd.memset(warm[:], 1.0)
         nc.scalar.activation(warm_out[:], warm[:], ACT.Abs_reciprocal_sqrt)
 
@@ -61,19 +59,19 @@ def tile_attend_cgroupscale_kernel(tc, tab_words, tab_scales, w1, gain, bias, wo
                 nc.sync.dma_start(scales[32 * q : 32 * q + 4, :].bitcast(I32), tab_scales[0, 4 * q : 4 * q + 4, :].bitcast(I32))
 
         nc.sync.dma_start(offsets[:], offs)
-        load_scales()
-        nc.sync.dma_start(w1_raw[:], w1.rearrange("(p t) r -> p t r", t=PACK))
         nc.sync.dma_start(words[:].bitcast(I32), tab_words[0].bitcast(I32))
+        nc.sync.dma_start(w1_raw[:], w1.rearrange("(p t) r -> p t r", t=PACK))
+        with nc.allow_non_contiguous_dma(reason="one value a partition"):
+            nc.scalar.dma_start(gain_sb[:], gain.rearrange("(h p) o -> p (h o)", p=P))
+            nc.scalar.dma_start(bias_sb[:], bias.rearrange("(h p) o -> p (h o)", p=P))
+        load_scales()
+        wo_raw = tile("wo_raw", [P, PACK, R], F32)
+        dy_all = tile("dy_raw", [P, NC, PACK * CW], F32)
+        dy_raw = [dy_all[:, c, :].rearrange("p (t j) -> p t j", t=PACK) for c in range(NC)]
         nc.sync.dma_start(wo_raw[:], wo.rearrange("(p t) r -> p t r", t=PACK))
         dy_v = dy.rearrange("(p t) j -> p t j", t=PACK)
         for c in range(NC):
-            nc.sync.dma_start(dy_raw[c][:], dy_v[:, :, c * CW : (c + 1) * CW])
-        with nc.allow_non_contiguous_dma(reason="one value a partition"):
-            nc.sync.dma_start(gain_sb[:], gain.rearrange("(h p) o -> p (h o)", p=P))
-            nc.sync.dma_start(bias_sb[:], bias.rearrange("(h p) o -> p (h o)", p=P))
-        old_v = old.rearrange("(h p) j -> p h j", p=P)
-        for c in range(NC):
-            nc.sync.dma_start(old_sb[c][:], old_v[:, :, c * CW : (c + 1) * CW])
+            nc.sync.dma_start(dy_raw[c], dy_v[:, :, c * CW : (c + 1) * CW])
 
         def quantize(name, grouped, width):
             codes = tile(name + "_codes", [P, width], U32)
@@ -81,25 +79,29 @@ def tile_attend_cgroupscale_kernel(tc, tab_words, tab_scales, w1, gain, bias, wo
             nc.vector.quantize_mx(codes[:].bitcast(FP8X4), plane[:], grouped[:].rearrange("p w t -> p (w t)"))
             return codes, plane
 
-        w1_bf = tile("w1_bf", [P, R, PACK], BF16)
-        interleave(nc.scalar.copy, w1_bf[:], w1_raw[:])
+        w1_bf = [tile(f"w1_bf{h}", [P, P, PACK], BF16) for h in range(H)]
+        interleave(nc.scalar.copy, w1_bf[0][:], w1_raw[:, :, :P])
         g_scales, g_words = [], []
-        for c in range(NC):
-            gs = tile(f"g_scales{c}", [P, CW], U8)
-            nc.vector.tensor_copy(gs[:], scales[:].indirect(offsets[:, c * CW // 16 : (c + 1) * CW // 16]))
-            g_scales.append(gs)
-        w1_codes, w1_plane = quantize("w1", w1_bf, R)
         for c in range(NC):
             gw = tile(f"g_words{c}", [P, CW], U16)
             nc.vector.tensor_copy(gw[:], words[:].indirect(offsets[:, c * CW // 16 : (c + 1) * CW // 16]))
             g_words.append(gw)
+        interleave(nc.vector.tensor_copy, w1_bf[1][:], w1_raw[:, :, P:])
+        old_sb = tile("old_sb", [P, H, J], F32, slot="w1_raw")
+        nc.sync.dma_start(old_sb[:], old.rearrange("(h p) j -> p h j", p=P))
+        for c in range(NC):
+            gs = tile(f"g_scales{c}", [P, CW], U8)
+            nc.vector.tensor_copy(gs[:], scales[:].indirect(offsets[:, c * CW // 16 : (c + 1) * CW // 16]))
+            g_scales.append(gs)
+            if c == 0:
+                w1_q = [quantize(f"w1{h}", w1_bf[h], P) for h in range(H)]
         a_ps = [ps.tile([P, H, CW], F32, name=f"a_ps{c}") for c in range(NC)]
         for c in range(NC):
             for h in range(H):
                 nc.tensor.matmul_mx(
                     a_ps[c][:, h, :],
-                    lhsT=w1_codes[:, h * P : (h + 1) * P].bitcast(FP8X4),
-                    lhsT_scale=w1_plane[:, h * P : (h + 1) * P],
+                    lhsT=w1_q[h][0][:].bitcast(FP8X4),
+                    lhsT_scale=w1_q[h][1][:],
                     rhs=g_words[c][:].bitcast(FP4X4),
                     rhs_scale=g_scales[c][:],
                     start=True,
@@ -110,22 +112,21 @@ def tile_attend_cgroupscale_kernel(tc, tab_words, tab_scales, w1, gain, bias, wo
         interleave(nc.scalar.copy, wo_bf[:], wo_raw[:])
         dy_bf = [tile(f"dy_bf{c}", [P, CW, PACK], BF16) for c in range(NC)]
         for c in range(NC):
-            interleave(nc.scalar.copy, dy_bf[c][:], dy_raw[c][:])
+            interleave(nc.scalar.copy, dy_bf[c][:], dy_raw[c])
 
         NG = H * CG
-        stats, rstd = [], []
+        stats_all = tile("stats", [P, NC * NG, 3], F32)
+        stats = [stats_all[:, c * NG : (c + 1) * NG, :] for c in range(NC)]
         for c in range(NC):
-            st = tile(f"stats{c}", [P, NG, 3], F32)
             flat = a_ps[c][:].rearrange("p h j -> p (h j)")
             for n in range(NG // 2):
                 nc.vector.bn_stats(
-                    st[:, 2 * n : 2 * n + 2, :].rearrange("p g s -> p (g s)"),
+                    stats[c][:, 2 * n : 2 * n + 2, :].rearrange("p g s -> p (g s)"),
                     flat[:, 2 * n * GS : (2 * n + 2) * GS].rearrange("p (g i) -> p i g", g=2),
                 )
-            rs = tile(f"rstd{c}", [P, NG], F32)
-            nc.scalar.activation(rs[:], st[:, :, 2], ACT.Abs_reciprocal_sqrt, bias=EPS, scale=1.0 / GS)
-            stats.append(st)
-            rstd.append(rs)
+        rstd_all = tile("rstd", [P, NC * NG], F32, slot="dy_raw")
+        nc.scalar.activation(rstd_all[:], stats_all[:, :, 2], ACT.Abs_reciprocal_sqrt, bias=EPS, scale=1.0 / GS)
+        rstd = [rstd_all[:, c * NG : (c + 1) * NG] for c in range(NC)]
 
         def by_group(ap):
             return ap.rearrange("p (g i) -> p g i", i=GS)
@@ -143,7 +144,7 @@ def tile_attend_cgroupscale_kernel(tc, tab_words, tab_scales, w1, gain, bias, wo
         xh = []
         for c in range(NC):
             x = tile(f"xh{c}", [P, H * CW], F32)
-            nc.vector.tensor_tensor(by_group(x[:]), by_group(ce[c][:]), spread(rstd[c][:]), ALU.mult)
+            nc.gpsimd.tensor_tensor(by_group(x[:]), by_group(ce[c][:]), spread(rstd[c]), ALU.mult)
             xh.append(x)
 
         wo_codes, wo_plane = quantize("wo", wo_bf, R)
@@ -197,7 +198,7 @@ def tile_attend_cgroupscale_kernel(tc, tab_words, tab_scales, w1, gain, bias, wo
         directs = {}
         for c, h in pieces:
             directs[c, h] = tile(f"direct{c}{h}", [P, CW], F32)
-            nc.vector.tensor_tensor(directs[c, h][:], old_sb[c][:, h, :], dps[c, h][:, 0, :], ALU.subtract)
+            nc.vector.tensor_tensor(directs[c, h][:], old_sb[:, h, c * CW : (c + 1) * CW], dps[c, h][:, 0, :], ALU.subtract)
         for c, h in pieces:
             y = tile(f"y{c}{h}", [P, CW], F32)
             nc.vector.scalar_tensor_tensor(y[:], backs[c, h][:], 1.0 / GS, directs[c, h][:], ALU.mult, ALU.add)

@@ -44,8 +44,6 @@ def tile_attend_cgroupscale_kernel(tc, tab_words, tab_scales, w1, gain, bias, wo
         words = tile("words", [P, T], U16)
         scales = tile("scales", [P, T], U8)
         w1_raw = tile("w1_raw", [P, PACK, R], F32)
-        gain_sb = tile("gain_sb", [P, H], F32)
-        bias_sb = tile("bias_sb", [P, H], F32)
 
         nc.gpsimd.memset(scales[:, : T // 2].bitcast(I32), 0)
         nc.vector.memset(scales[:, T // 2 :].bitcast(I32), 0)
@@ -61,9 +59,6 @@ def tile_attend_cgroupscale_kernel(tc, tab_words, tab_scales, w1, gain, bias, wo
         nc.sync.dma_start(offsets[:], offs)
         nc.sync.dma_start(words[:].bitcast(I32), tab_words[0].bitcast(I32))
         nc.sync.dma_start(w1_raw[:], w1.rearrange("(p t) r -> p t r", t=PACK))
-        with nc.allow_non_contiguous_dma(reason="one value a partition"):
-            nc.scalar.dma_start(gain_sb[:], gain.rearrange("(h p) o -> p (h o)", p=P))
-            nc.scalar.dma_start(bias_sb[:], bias.rearrange("(h p) o -> p (h o)", p=P))
         load_scales()
         wo_raw = tile("wo_raw", [P, PACK, R], F32)
         dy_all = tile("dy_raw", [P, NC, PACK * CW], F32)
@@ -95,6 +90,11 @@ def tile_attend_cgroupscale_kernel(tc, tab_words, tab_scales, w1, gain, bias, wo
             g_scales.append(gs)
             if c == 0:
                 w1_q = [quantize(f"w1{h}", w1_bf[h], P) for h in range(H)]
+        gain_sb = tile("gain_sb", [P, H], F32, slot="w1_bf0")
+        bias_sb = tile("bias_sb", [P, H], F32, slot="w1_bf1")
+        with nc.allow_non_contiguous_dma(reason="one value a partition"):
+            nc.sync.dma_start(gain_sb[:], gain.rearrange("(h p) o -> p (h o)", p=P))
+            nc.sync.dma_start(bias_sb[:], bias.rearrange("(h p) o -> p (h o)", p=P))
         a_ps = [ps.tile([P, H, CW], F32, name=f"a_ps{c}") for c in range(NC)]
         for c in range(NC):
             for h in range(H):
@@ -124,29 +124,6 @@ def tile_attend_cgroupscale_kernel(tc, tab_words, tab_scales, w1, gain, bias, wo
                     stats[c][:, 2 * n : 2 * n + 2, :].rearrange("p g s -> p (g s)"),
                     flat[:, 2 * n * GS : (2 * n + 2) * GS].rearrange("p (g i) -> p i g", g=2),
                 )
-        rstd_all = tile("rstd", [P, NC * NG], F32, slot="dy_raw")
-        nc.scalar.activation(rstd_all[:], stats_all[:, :, 2], ACT.Abs_reciprocal_sqrt, bias=EPS, scale=1.0 / GS)
-        rstd = [rstd_all[:, c * NG : (c + 1) * NG] for c in range(NC)]
-
-        def by_group(ap):
-            return ap.rearrange("p (g i) -> p g i", i=GS)
-
-        def spread(ap):
-            return ap.unsqueeze(2).to_broadcast([P, ap.shape[1], GS])
-
-        ce = []
-        for c in range(NC):
-            t = tile(f"ce{c}", [P, H * CW], F32)
-            nc.vector.tensor_tensor(
-                by_group(t[:]), by_group(a_ps[c][:].rearrange("p h j -> p (h j)")), spread(stats[c][:, :, 1]), ALU.subtract
-            )
-            ce.append(t)
-        xh = []
-        for c in range(NC):
-            x = tile(f"xh{c}", [P, H * CW], F32)
-            nc.gpsimd.tensor_tensor(by_group(x[:]), by_group(ce[c][:]), spread(rstd[c]), ALU.mult)
-            xh.append(x)
-
         wo_codes, wo_plane = quantize("wo", wo_bf, R)
         c_ps = [ps.tile([P, H, CW], F32, name=f"c_ps{c}") for c in range(NC)]
         for c in range(NC):
@@ -162,14 +139,30 @@ def tile_attend_cgroupscale_kernel(tc, tab_words, tab_scales, w1, gain, bias, wo
                     stop=True,
                 )
 
+        rstd_all = tile("rstd", [P, NC * NG], F32, slot="dy_raw")
+        nc.scalar.activation(rstd_all[:], stats_all[:, :, 2], ACT.Abs_reciprocal_sqrt, bias=EPS, scale=1.0 / GS)
+        rstd = [rstd_all[:, c * NG : (c + 1) * NG] for c in range(NC)]
+
+        def by_group(ap):
+            return ap.rearrange("p (g i) -> p g i", i=GS)
+
+        def spread(ap):
+            return ap.unsqueeze(2).to_broadcast([P, ap.shape[1], GS])
+
+        ce_all = tile("ce", [P, NC, H * CW], F32, slot=f"dy_bf{NC - 1}")
+        xh = [tile(f"xh{c}", [P, H * CW], F32) for c in range(NC)]
+        for c in range(NC):
+            for h in range(H):
+                cols = slice(h * CW, (h + 1) * CW)
+                groups = slice(h * CG, (h + 1) * CG)
+                nc.vector.tensor_tensor(
+                    by_group(ce_all[:, c, cols]), by_group(a_ps[c][:, h, :]), spread(stats[c][:, groups, 1]), ALU.subtract
+                )
+                if (c, h) != (NC - 1, H - 1):
+                    nc.gpsimd.tensor_tensor(by_group(xh[c][:, cols]), by_group(ce_all[:, c, cols]), spread(rstd[c][:, groups]), ALU.mult)
+
         pieces = [(c, h) for c in range(NC) for h in range(H)]
         u2, scaled = {}, {}
-        for c, h in pieces:
-            cols = slice(h * CW, (h + 1) * CW)
-            u = tile(f"u{c}{h}", [P, CW], F32)
-            nc.scalar.activation(u[:], xh[c][:, cols], ACT.Tanh, bias=bias_sb[:, h : h + 1], scale=gain_sb[:, h : h + 1])
-            u2[c, h] = tile(f"u2{c}{h}", [P, CW], F32)
-            nc.scalar.activation(u2[c, h][:], u[:], ACT.Square)
         for c, h in pieces:
             scaled[c, h] = tile(f"cs{c}{h}", [P, CW], F32)
             nc.vector.scalar_tensor_tensor(
@@ -180,6 +173,15 @@ def tile_attend_cgroupscale_kernel(tc, tab_words, tab_scales, w1, gain, bias, wo
                 ALU.mult,
                 ALU.mult,
             )
+        nc.vector.tensor_tensor(
+            by_group(xh[NC - 1][:, CW:]), by_group(ce_all[:, NC - 1, CW:]), spread(rstd[NC - 1][:, CG:]), ALU.mult
+        )
+        for c, h in pieces:
+            cols = slice(h * CW, (h + 1) * CW)
+            u = tile(f"u{c}{h}", [P, CW], F32)
+            nc.scalar.activation(u[:], xh[c][:, cols], ACT.Tanh, bias=bias_sb[:, h : h + 1], scale=gain_sb[:, h : h + 1])
+            u2[c, h] = tile(f"u2{c}{h}", [P, CW], F32)
+            nc.scalar.activation(u2[c, h][:], u[:], ACT.Square)
         dps, backs = {}, {}
         for c, h in pieces:
             x = xh[c][:, h * CW : (h + 1) * CW]

from contextlib import ExitStack

import concourse.mybir as mybir

K, R, F, T, J = 512, 256, 512, 2048, 512
FLOPS = 2 * K * R * J + 2 * F * R * J

F32 = mybir.dt.float32
BF16 = mybir.dt.bfloat16
I32 = mybir.dt.int32
U32 = mybir.dt.uint32
U16 = mybir.dt.uint16
U8 = mybir.dt.uint8
FP8X4 = mybir.dt.float8_e4m3fn_x4
FP4X4 = mybir.dt.float4_e2m1fn_x4
ALU = mybir.AluOpType
ACT = mybir.ActivationFunctionType
AX = mybir.AxisListType

P = 128
PACK = 4
H = R // P
GS = 16
NC = 2
CW = J // NC
CG = CW // GS
EPS = 0.05


def interleave(engine_copy, dst, src):
    engine_copy(dst.rearrange("p (c i) t -> p c t i", i=4), src.rearrange("p t (c i) -> p c t i", i=4))


def tile_attend_cgroupscale_kernel(tc, tab_words, tab_scales, w1, gain, bias, wo, dy, old, offs, out):
    nc = tc.nc
    with ExitStack() as ctx:
        sb = ctx.enter_context(tc.tile_pool(name="sb", bufs=1))
        ps = ctx.enter_context(tc.psum_pool(name="ps", bufs=1))

        def tile(name, shape, dtype, slot=None):
            return sb.tile(shape, dtype, name=name, tag=slot or name, align_bytes=64)

        offsets = sb.tile([P, J // 16], U16, name="offsets")
        words = tile("words", [P, T], U16)
        scales = tile("scales", [P, T], U8)
        w1_raw = tile("w1_raw", [P, PACK, R], F32)

        nc.gpsimd.memset(scales[:, : T // 2].bitcast(I32), 0)
        nc.vector.memset(scales[:, T // 2 :].bitcast(I32), 0)
        warm = tile("warm", [P, 1], F32, slot="wo_raw")
        warm_out = tile("warm_out", [P, 1], F32, slot="dy_raw")
        nc.gpsimd.memset(warm[:], 1.0)
        nc.scalar.activation(warm_out[:], warm[:], ACT.Abs_reciprocal_sqrt)

        def load_scales():
            for q in range(4):
                nc.sync.dma_start(scales[32 * q : 32 * q + 4, :].bitcast(I32), tab_scales[0, 4 * q : 4 * q + 4, :].bitcast(I32))

        nc.sync.dma_start(offsets[:], offs)
        nc.sync.dma_start(words[:].bitcast(I32), tab_words[0].bitcast(I32))
        nc.sync.dma_start(w1_raw[:], w1.rearrange("(p t) r -> p t r", t=PACK))
        load_scales()
        wo_raw = tile("wo_raw", [P, PACK, R], F32)
        dy_all = tile("dy_raw", [P, NC, PACK * CW], F32)
        dy_raw = [dy_all[:, c, :].rearrange("p (t j) -> p t j", t=PACK) for c in range(NC)]
        nc.sync.dma_start(wo_raw[:], wo.rearrange("(p t) r -> p t r", t=PACK))
        dy_v = dy.rearrange("(p t) j -> p t j", t=PACK)
        for c in range(NC):
            nc.sync.dma_start(dy_raw[c], dy_v[:, :, c * CW : (c + 1) * CW])

        def quantize(name, grouped, width):
            codes = tile(name + "_codes", [P, width], U32)
            plane = tile(name + "_plane", [P, width], U8)
            nc.vector.quantize_mx(codes[:].bitcast(FP8X4), plane[:], grouped[:].rearrange("p w t -> p (w t)"))
            return codes, plane

        w1_bf = [tile(f"w1_bf{h}", [P, P, PACK], BF16) for h in range(H)]
        interleave(nc.scalar.copy, w1_bf[0][:], w1_raw[:, :, :P])
        g_scales, g_words = [], []
        for c in range(NC):
            gw = tile(f"g_words{c}", [P, CW], U16)
            nc.vector.tensor_copy(gw[:], words[:].indirect(offsets[:, c * CW // 16 : (c + 1) * CW // 16]))
            g_words.append(gw)
        interleave(nc.vector.tensor_copy, w1_bf[1][:], w1_raw[:, :, P:])
        old_sb = tile("old_sb", [P, H, J], F32, slot="w1_raw")
        nc.sync.dma_start(old_sb[:], old.rearrange("(h p) j -> p h j", p=P))
        for c in range(NC):
            gs = tile(f"g_scales{c}", [P, CW], U8)
            nc.vector.tensor_copy(gs[:], scales[:].indirect(offsets[:, c * CW // 16 : (c + 1) * CW // 16]))
            g_scales.append(gs)
            if c == 0:
                w1_q = [quantize(f"w1{h}", w1_bf[h], P) for h in range(H)]
        gain_sb = tile("gain_sb", [P, H], F32, slot="w1_bf0")
        bias_sb = tile("bias_sb", [P, H], F32, slot="w1_bf1")
        with nc.allow_non_contiguous_dma(reason="one value a partition"):
            nc.sync.dma_start(gain_sb[:], gain.rearrange("(h p) o -> p (h o)", p=P))
            nc.sync.dma_start(bias_sb[:], bias.rearrange("(h p) o -> p (h o)", p=P))
        a_ps = [ps.tile([P, H, CW], F32, name=f"a_ps{c}") for c in range(NC)]
        for c in range(NC):
            for h in range(H):
                nc.tensor.matmul_mx(
                    a_ps[c][:, h, :],
                    lhsT=w1_q[h][0][:].bitcast(FP8X4),
                    lhsT_scale=w1_q[h][1][:],
                    rhs=g_words[c][:].bitcast(FP4X4),
                    rhs_scale=g_scales[c][:],
                    start=True,
                    stop=True,
                )

        wo_bf = tile("wo_bf", [P, R, PACK], BF16)
        interleave(nc.scalar.copy, wo_bf[:], wo_raw[:])
        dy_bf = [tile(f"dy_bf{c}", [P, CW, PACK], BF16) for c in range(NC)]
        for c in range(NC):
            interleave(nc.scalar.copy, dy_bf[c][:], dy_raw[c])

        NG = H * CG
        stats_all = tile("stats", [P, NC * NG, 3], F32)
        stats = [stats_all[:, c * NG : (c + 1) * NG, :] for c in range(NC)]
        for c in range(NC):
            flat = a_ps[c][:].rearrange("p h j -> p (h j)")
            for n in range(NG // 2):
                nc.vector.bn_stats(
                    stats[c][:, 2 * n : 2 * n + 2, :].rearrange("p g s -> p (g s)"),
                    flat[:, 2 * n * GS : (2 * n + 2) * GS].rearrange("p (g i) -> p i g", g=2),
                )
        wo_codes, wo_plane = quantize("wo", wo_bf, R)
        c_ps = [ps.tile([P, H, CW], F32, name=f"c_ps{c}") for c in range(NC)]
        for c in range(NC):
            dy_codes, dy_plane = quantize(f"dy{c}", dy_bf[c], CW)
            for h in range(H):
                nc.tensor.matmul_mx(
                    c_ps[c][:, h, :],
                    lhsT=wo_codes[:, h * P : (h + 1) * P].bitcast(FP8X4),
                    lhsT_scale=wo_plane[:, h * P : (h + 1) * P],
                    rhs=dy_codes[:].bitcast(FP8X4),
                    rhs_scale=dy_plane[:],
                    start=True,
                    stop=True,
                )

        rstd_all = tile("rstd", [P, NC * NG], F32, slot="dy_raw")
        nc.scalar.activation(rstd_all[:], stats_all[:, :, 2], ACT.Abs_reciprocal_sqrt, bias=EPS, scale=1.0 / GS)
        rstd = [rstd_all[:, c * NG : (c + 1) * NG] for c in range(NC)]

        def by_group(ap):
            return ap.rearrange("p (g i) -> p g i", i=GS)

        def spread(ap):
            return ap.unsqueeze(2).to_broadcast([P, ap.shape[1], GS])

        ce_all = tile("ce", [P, NC, H * CW], F32, slot=f"dy_bf{NC - 1}")
        xh = [tile(f"xh{c}", [P, H * CW], F32) for c in range(NC)]
        for c in range(NC):
            for h in range(H):
                cols = slice(h * CW, (h + 1) * CW)
                groups = slice(h * CG, (h + 1) * CG)
                nc.vector.tensor_tensor(
                    by_group(ce_all[:, c, cols]), by_group(a_ps[c][:, h, :]), spread(stats[c][:, groups, 1]), ALU.subtract
                )
                if (c, h) != (NC - 1, H - 1):
                    nc.gpsimd.tensor_tensor(by_group(xh[c][:, cols]), by_group(ce_all[:, c, cols]), spread(rstd[c][:, groups]), ALU.mult)

        pieces = [(c, h) for c in range(NC) for h in range(H)]
        u2, scaled = {}, {}
        for c, h in pieces:
            scaled[c, h] = tile(f"cs{c}{h}", [P, CW], F32)
            nc.vector.scalar_tensor_tensor(
                by_group(scaled[c, h][:]),
                by_group(c_ps[c][:, h, :]),
                gain_sb[:, h : h + 1],
                spread(rstd[c][:, h * CG : (h + 1) * CG]),
                ALU.mult,
                ALU.mult,
            )
        nc.vector.tensor_tensor(
            by_group(xh[NC - 1][:, CW:]), by_group(ce_all[:, NC - 1, CW:]), spread(rstd[NC - 1][:, CG:]), ALU.mult
        )
        for c, h in pieces:
            cols = slice(h * CW, (h + 1) * CW)
            u = tile(f"u{c}{h}", [P, CW], F32)
            nc.scalar.activation(u[:], xh[c][:, cols], ACT.Tanh, bias=bias_sb[:, h : h + 1], scale=gain_sb[:, h : h + 1])
            u2[c, h] = tile(f"u2{c}{h}", [P, CW], F32)
            nc.scalar.activation(u2[c, h][:], u[:], ACT.Square)
        dps, backs = {}, {}
        for c, h in pieces:
            x = xh[c][:, h * CW : (h + 1) * CW]
            dp = tile(f"dp{c}{h}", [P, 2, CW], F32)
            nc.vector.scalar_tensor_tensor(dp[:, 0, :], u2[c, h][:], -1.0, scaled[c, h][:], ALU.add, ALU.mult)
            nc.vector.tensor_tensor(dp[:, 1, :], dp[:, 0, :], x, ALU.mult)
            sums = tile(f"sums{c}{h}", [P, 2 * CG], F32)
            nc.vector.tensor_reduce(sums[:], dp[:].rearrange("p q (g i) -> p (q g) i", i=GS), AX.X, ALU.add)
            back = tile(f"back{c}{h}", [P, CW], F32)
            for g in range(CG):
                cols = slice(g * GS, (g + 1) * GS)
                nc.scalar.activation(
                    back[:, cols], x[:, cols], ACT.Identity, bias=sums[:, g : g + 1], scale=sums[:, CG + g : CG + g + 1]
                )
            dps[c, h], backs[c, h] = dp, back
        directs = {}
        for c, h in pieces:
            directs[c, h] = tile(f"direct{c}{h}", [P, CW], F32)
            nc.vector.tensor_tensor(directs[c, h][:], old_sb[:, h, c * CW : (c + 1) * CW], dps[c, h][:, 0, :], ALU.subtract)
        for c, h in pieces:
            y = tile(f"y{c}{h}", [P, CW], F32)
            nc.vector.scalar_tensor_tensor(y[:], backs[c, h][:], 1.0 / GS, directs[c, h][:], ALU.mult, ALU.add)
            nc.sync.dma_start(out[h * P : (h + 1) * P, c * CW : (c + 1) * CW], y[:])
